import numpy as np
import ml_dtypes


def mxq(x, axis, fmt="e4m3"):
    dtype, down = {"e4m3": (ml_dtypes.float8_e4m3fn, 7), "e5m2": (ml_dtypes.float8_e5m2, 14)}[fmt]
    v = np.moveaxis(np.asarray(x, np.float32).astype(ml_dtypes.bfloat16).astype(np.float64), axis, -1)
    blocks = v.reshape(v.shape[:-1] + (-1, 32))
    amax = np.abs(blocks).max(-1, keepdims=True)
    byte = np.maximum(np.where(amax > 0, np.frexp(amax)[1] - 1 + 127, 0) - down, 1)
    scale = np.exp2(byte - 127.0)
    codes = (blocks / scale).astype(np.float32).astype(dtype).astype(np.float64)
    return np.moveaxis((codes * scale).reshape(v.shape), -1, axis)


WIDE = False


def mx_kscale(k):
    if not WIDE:
        return np.ones(k)
    levels = np.array([10, -10, 5, -5, 0])
    if k % 512:
        return np.exp2(np.random.permutation(np.resize(levels, k // 32))).repeat(32)
    a = np.empty((k // 512, 16))
    for p in range(k // 512):
        a[p, :8] = np.random.permutation(np.resize(levels, 8))
        for g in range(8):
            far = levels[np.abs(levels - a[p, g]) >= 10]
            a[p, g + 8] = far[np.random.randint(len(far))]
    return np.exp2(a.ravel()).repeat(32)


def f64(x):
    return np.asarray(x).astype(np.float64)


def striped(idx):
    return np.tile(np.asarray(idx).reshape(-1, 16).T, (8, 1)).astype(np.uint16)


def unstriped(offs):
    return offs[:16].T.reshape(-1).astype(np.int64)


E2M1 = np.array([0.0, 0.5, 1.0, 1.5, 2.0, 3.0, 4.0, 6.0, -0.0, -0.5, -1.0, -1.5, -2.0, -3.0, -4.0, -6.0])


def pack_weight(w, fmt):
    k, n = w.shape
    w = f64(np.asarray(w, np.float32).astype(ml_dtypes.bfloat16)).reshape(k // 32, 32, n)
    amax = np.abs(w).max(1)
    if fmt == "e4m3":
        byte = np.frexp(amax)[1] - 1 + 127 - 7
    else:
        mant, ex = np.frexp(amax / 6.0)
        byte = np.where(mant > 0.5, ex, ex - 1) + 127
    byte = np.clip(np.where(amax > 0, byte, 1), 1, 254)
    scaled = (w * np.exp2(127.0 - byte)[:, None, :]).reshape(k, n).astype(np.float32)
    by_word = np.ascontiguousarray(scaled.reshape(k // 512, 128, 4, n).transpose(0, 1, 3, 2))
    if fmt == "e4m3":
        words = by_word.astype(ml_dtypes.float8_e4m3fn).view(np.uint8)
    else:
        c = by_word.astype(ml_dtypes.float4_e2m1fn).view(np.uint8) & 0xF
        words = (c[..., 0::2] | (c[..., 1::2] << 4)).reshape(k // 512, 128, 2 * n)
    return np.ascontiguousarray(words), np.ascontiguousarray(byte.astype(np.uint8).reshape(k // 512, 16, n))


def unpack_weight(words, scales, fmt):
    g, _, n = scales.shape
    words = np.ascontiguousarray(words).reshape(g, 128, n, -1)
    if fmt == "e4m3":
        vals = words.view(ml_dtypes.float8_e4m3fn).astype(np.float64)
    else:
        nib = np.empty((g, 128, n, 4), np.uint8)
        nib[..., 0::2] = words & 0xF
        nib[..., 1::2] = words >> 4
        vals = E2M1[nib]
    vals = vals * np.repeat(np.exp2(scales.astype(np.float64) - 127.0), 8, axis=1)[..., None]
    return vals.transpose(0, 1, 3, 2).reshape(g * 512, n)


def softplus(v):
    return np.log(1.0 + np.exp(v))


def sigmoid(v):
    return 1.0 / (1.0 + np.exp(-v))


D, E, T, I, Q, G = 512, 512, 2048, 512, 128, 32


def setup_inputs():
    n = np.random.standard_normal
    idx = np.random.permutation(T)[:I]
    fd = mx_kscale(D)
    fe = mx_kscale(E)
    keysp = pack_weight(n((D, T)) / fd[:, None], "e4m3")
    valsp = pack_weight(n((E, T)) / fe[:, None], "e4m3")
    return {
        "query": (n((D, Q)) * 1.0 / np.sqrt(D) * fd[:, None]).astype(np.float32),
        "keys_words": keysp[0],
        "keys_scales": keysp[1],
        "margin": (np.random.uniform(-0.5, 0.5, (Q, 1))).astype(np.float32),
        "reserve": (np.random.uniform(5.0, 20.0, (Q, 1))).astype(np.float32),
        "gout": (n((E, Q)) * 1 / np.sqrt(E) * fe[:, None]).astype(np.float32),
        "vals_words": valsp[0],
        "vals_scales": valsp[1],
        "old": (0.5 * n((Q, T))).astype(np.float32),
        "offs": striped(idx),
    }


def reference(query, keys_words, keys_scales, margin, reserve, gout, vals_words, vals_scales, old, offs):
    idx = unstriped(offs)
    keysu = unpack_weight(keys_words, keys_scales, "e4m3")
    valsu = unpack_weight(vals_words, vals_scales, "e4m3")
    queryq = mxq(f64(query), 0, "e4m3")
    keysidxg = keysu[:, idx]
    a = queryq.T @ keysidxg
    m1 = a.reshape(Q, G, I // G).mean(axis=2)
    mr = np.repeat(m1, I // G, axis=1)
    p = softplus(a - mr - f64(margin))
    n2 = np.sqrt(np.sum(np.square(p), axis=1, keepdims=True) + f64(reserve))
    goutq = mxq(f64(gout), 0, "e4m3")
    valsidxg = valsu[:, idx]
    c0 = goutq.T @ valsidxg
    dn2 = np.sum(c0 * p / np.square(n2) * (-1.0), axis=1, keepdims=True)
    dp = c0 / n2 + dn2 * 0.5 / np.sqrt(np.sum(np.square(p), axis=1, keepdims=True) + f64(reserve)) * p * 2.0
    dmr = dp * sigmoid(a - mr - f64(margin)) * (-1.0)
    dm1 = dmr.reshape(Q, G, I // G).sum(axis=2)
    e1 = dm1 / 16.0
    r1 = np.repeat(e1, I // G, axis=1)
    da = dp * sigmoid(a - mr - f64(margin)) + r1
    gs = da * 16.0
    gf = np.zeros((Q, T))
    gf[:, idx] = gs
    y = f64(old) + gf
    return y

@@ -1,0 +1,151 @@
+from contextlib import ExitStack
+
+import concourse.mybir as mybir
+
+D, T, I, Q = 512, 2048, 512, 128
+FLOPS = 2 * 2 * D * Q * I
+
+F32 = mybir.dt.float32
+BF16 = mybir.dt.bfloat16
+I32 = mybir.dt.int32
+U32 = mybir.dt.uint32
+U16 = mybir.dt.uint16
+U8 = mybir.dt.uint8
+FP8X4 = mybir.dt.float8_e4m3fn_x4
+ALU = mybir.AluOpType
+ACT = mybir.ActivationFunctionType
+AX = mybir.AxisListType
+
+P = 128
+PAGE = 16
+HALF = I // 2
+HP = HALF // PAGE
+CAP = 16.0
+VPLANE = 4
+OUT_CUTS = (0, 256, 768, 1280, 1792, 2048)
+
+
+def tile_attend_bsharedthreshold_s_kernel(tc, query, keys_words, keys_scales, margin, reserve, gout, vals_words, vals_scales, old, offs, out):
+    nc = tc.nc
+    with ExitStack() as ctx:
+        sb = ctx.enter_context(tc.tile_pool(name="sb", bufs=1))
+        ps = ctx.enter_context(tc.psum_pool(name="ps", bufs=1))
+
+        offsets = sb.tile([P, I // 16], U16, name="offsets")
+        k_bytes = sb.tile([P, T], U8, name="k_bytes")
+        v_bytes = sb.tile([P, T], U8, name="v_bytes")
+        k_words = sb.tile([P, T], U32, name="k_words")
+        v_words = sb.tile([P, T], U32, name="v_words")
+        q_raw = sb.tile([P, 4, Q], F32, name="q_raw")
+        g_raw = sb.tile([P, 4, Q], F32, name="g_raw")
+        acc = sb.tile([P, T], F32, name="acc")
+        placed = sb.tile([P, T], F32, name="placed")
+        margin_sb = sb.tile([P, 1], F32, name="margin_sb")
+        reserve_sb = sb.tile([P, 1], F32, name="reserve_sb")
+        neg_cap = sb.tile([P, 1], F32, name="neg_cap")
+
+        nc.vector.memset(k_bytes[:].bitcast(I32), 0)
+        nc.vector.memset(v_bytes[:].bitcast(I32), 0)
+        nc.vector.memset(neg_cap[:], -CAP)
+        nc.vector.memset(placed[:], 0.0)
+
+        nc.sync.dma_start(offsets[:], offs)
+        nc.sync.dma_start(q_raw[:], query.rearrange("(p j) w -> p j w", j=4))
+        for r in range(4):
+            nc.scalar.dma_start(k_bytes[32 * r : 32 * r + 4, :].bitcast(I32), keys_scales[0, 4 * r : 4 * r + 4, :].bitcast(I32))
+        nc.sync.dma_start(k_words[:].bitcast(I32), keys_words[0].rearrange("p n t -> p (n t)").bitcast(I32))
+        nc.sync.dma_start(g_raw[:], gout.rearrange("(p j) w -> p j w", j=4))
+        nc.sync.dma_start(v_words[:].bitcast(I32), vals_words[0].rearrange("p n t -> p (n t)").bitcast(I32))
+        nc.sync.dma_start(acc[:], old)
+        nc.gpsimd.dma_start(margin_sb[:], margin)
+        for r in range(4):
+            nc.gpsimd.dma_start(v_bytes[32 * r + VPLANE : 32 * r + VPLANE + 4, :].bitcast(I32), vals_scales[0, 4 * r : 4 * r + 4, :].bitcast(I32))
+        nc.gpsimd.dma_start(reserve_sb[:], reserve)
+
+        def quantise(raw, name):
+            grouped = sb.tile([P, Q, 4], BF16, name=name + "_grouped", align_bytes=64)
+            codes = sb.tile([P, Q], U32, name=name + "_codes", align_bytes=64)
+            scales = sb.tile([P, Q], U8, name=name + "_scales", align_bytes=64)
+            nc.scalar.copy(grouped[:], raw[:].rearrange("p j w -> p w j"))
+            nc.vector.quantize_mx(codes[:].bitcast(FP8X4), scales[:], grouped[:].rearrange("p w j -> p (w j)"))
+            return codes, scales
+
+        halves = [slice(h * HALF, (h + 1) * HALF) for h in range(2)]
+        pages = [slice(h * HP, (h + 1) * HP) for h in range(2)]
+
+        def by_page(ap):
+            return ap.rearrange("p (g i) -> p g i", i=PAGE)
+
+        def spread(ap):
+            return ap.unsqueeze(2).to_broadcast([P, HP, PAGE])
+
+        kg_bytes = sb.tile([P, I], U8, name="kg_bytes", align_bytes=64)
+        vg_bytes = sb.tile([P, I], U8, name="vg_bytes", align_bytes=64)
+        kg_words = sb.tile([P, I], U32, name="kg_words", align_bytes=64)
+        vg_words = sb.tile([P, I], U32, name="vg_words", align_bytes=64)
+        margin_cap = sb.tile([P, 1], F32, name="margin_cap")
+        a_ps = [ps.tile([P, HALF], F32, name="a_ps%d" % h) for h in range(2)]
+        c_ps = ps.tile([P, I], F32, name="c_ps")
+        a_sum = sb.tile([P, 2 * HP], F32, name="a_sum")
+        w = sb.tile([P, I], F32, name="w")
+        y = sb.tile([P, I], F32, name="y")
+        g = sb.tile([P, I], F32, name="g")
+
+        nc.vector.tensor_copy(kg_bytes[:], k_bytes[:].indirect(offsets[:]))
+        q_codes, q_scales = quantise(q_raw, "q")
+        nc.vector.tensor_scalar_add(margin_cap[:], margin_sb[:], CAP)
+        for h in range(2):
+            nc.vector.tensor_copy(kg_words[:, halves[h]], k_words[:].indirect(offsets[:, pages[h]]))
+            nc.tensor.matmul_mx(a_ps[h][:], lhsT=q_codes[:].bitcast(FP8X4), lhsT_scale=q_scales[:],
+                                rhs=kg_words[:, halves[h]].bitcast(FP8X4), rhs_scale=kg_bytes[:, halves[h]], start=True, stop=True)
+        g_codes, g_scales = quantise(g_raw, "g")
+        for h in range(2):
+            nc.vector.tensor_reduce(a_sum[:, pages[h]], by_page(a_ps[h][:]), AX.X, ALU.add)
+            nc.vector.scalar_tensor_tensor(by_page(w[:, halves[h]]), spread(a_sum[:, pages[h]]), 1.0 / PAGE, by_page(a_ps[h][:]), ALU.mult, ALU.subtract)
+            nc.scalar.activation(y[:, halves[h]], w[:, halves[h]], ACT.Relu, bias=margin_cap[:])
+            nc.scalar.activation(g[:, halves[h]], y[:, halves[h]], ACT.Sigmoid, bias=neg_cap[:])
+
+        nc.vector.tensor_copy(vg_bytes[:], v_bytes[:].indirect(offsets[:]))
+        nc.vector.tensor_copy(vg_words[:], v_words[:].indirect(offsets[:]))
+        nc.tensor.matmul_mx(c_ps[:], lhsT=g_codes[:].bitcast(FP8X4), lhsT_scale=g_scales[:],
+                            rhs=vg_words[:].bitcast(FP8X4), rhs_scale=vg_bytes[VPLANE:P, :], start=True, stop=True)
+
+        pn = sb.tile([P, I], F32, name="pn")
+        sq = sb.tile([P, I], F32, name="sq")
+        cs = sb.tile([P, I], F32, name="cs")
+        pp = sb.tile([P, I], F32, name="pp")
+        u = sb.tile([P, I], F32, name="u")
+        cp = sb.tile([P, I], F32, name="cp")
+        mean = sb.tile([P, I], F32, name="mean")
+        s_part = [sb.tile([P, 1], F32, name="s_part%d" % h) for h in range(2)]
+        s_all = sb.tile([P, 1], F32, name="s_all")
+        rec = sb.tile([P, 1], F32, name="rec")
+        cp_sum = sb.tile([P, 1], F32, name="cp_sum")
+        kn = sb.tile([P, 1], F32, name="kn")
+        u_sum = sb.tile([P, 2 * HP], F32, name="u_sum")
+
+        nc.vector.scalar_tensor_tensor(cs[:], g[:], 1.0, c_ps[:], ALU.subtract, ALU.mult)
+        for h in range(2):
+            nc.scalar.activation(y[:, halves[1 - h]], g[:, halves[h]], ACT.Ln)
+        for h in range(2):
+            nc.vector.scalar_tensor_tensor(pn[:, halves[h]], w[:, halves[h]], margin_sb[:], y[:, halves[1 - h]], ALU.add, ALU.min)
+            nc.scalar.activation(sq[:, halves[h]], pn[:, halves[h]], ACT.Square, accum_out=s_part[h][:])
+        nc.vector.scalar_tensor_tensor(cp[:], pn[:], 1.0, c_ps[:], ALU.mult, ALU.mult, accum_out=cp_sum[:])
+        nc.vector.tensor_scalar(s_all[:], s_part[0][:], s_part[1][:], reserve_sb[:], ALU.add, ALU.add)
+        nc.vector.scalar_tensor_tensor(pp[:, halves[0]], g[:, halves[0]], 1.0, pn[:, halves[0]], ALU.subtract, ALU.mult)
+        nc.vector.reciprocal(rec[:], s_all[:])
+        nc.vector.scalar_tensor_tensor(pp[:, halves[1]], g[:, halves[1]], 1.0, pn[:, halves[1]], ALU.subtract, ALU.mult)
+        nc.vector.tensor_tensor(kn[:], cp_sum[:], rec[:], ALU.mult)
+        for h in range(2):
+            nc.vector.scalar_tensor_tensor(u[:, halves[h]], pp[:, halves[h]], kn[:], cs[:, halves[h]], ALU.mult, ALU.subtract)
+        for h in range(2):
+            nc.vector.tensor_reduce(u_sum[:, pages[h]], by_page(u[:, halves[h]]), AX.X, ALU.add)
+            nc.scalar.activation(by_page(mean[:, halves[h]]), spread(u_sum[:, pages[h]]), ACT.Copy, scale=-1.0 / PAGE)
+        alpha = u_sum[:, 2 * HP - 1 : 2 * HP]
+        nc.scalar.activation(alpha, rec[:], ACT.Sqrt, scale=256.0)
+        for h in range(2):
+            nc.vector.tensor_tensor(placed[:].indirect(offsets[:, pages[h]]), u[:, halves[h]], mean[:, halves[h]], ALU.add)
+        for c in range(len(OUT_CUTS) - 1):
+            cols = slice(OUT_CUTS[c], OUT_CUTS[c + 1])
+            nc.vector.scalar_tensor_tensor(acc[:, cols], placed[:, cols], alpha, acc[:, cols], ALU.mult, ALU.add)
+            nc.sync.dma_start(out[:, cols], acc[:, cols])

@@ -20,7 +20,8 @@ P = 128
 PAGE = 16
 HALF = I // 2
 HP = HALF // PAGE
-CAP = 16.0
+TINY = 2.0**-60
+LN_CUT = HALF + 2 * PAGE
 VPLANE = 4
 OUT_CUTS = (0, 256, 768, 1280, 1792, 2048)
 
@@ -34,20 +35,19 @@ def tile_attend_bsharedthreshold_s_kernel(tc, query, keys_words, keys_scales, ma
         offsets = sb.tile([P, I // 16], U16, name="offsets")
         k_bytes = sb.tile([P, T], U8, name="k_bytes")
         v_bytes = sb.tile([P, T], U8, name="v_bytes")
-        k_words = sb.tile([P, T], U32, name="k_words")
-        v_words = sb.tile([P, T], U32, name="v_words")
-        q_raw = sb.tile([P, 4, Q], F32, name="q_raw")
+        k_words = sb.tile([P, T], U32, name="k_words", tag="k_then_old")
+        q_raw = sb.tile([P, 4, Q], F32, name="q_raw", tag="q_then_v")
         g_raw = sb.tile([P, 4, Q], F32, name="g_raw")
-        acc = sb.tile([P, T], F32, name="acc")
         placed = sb.tile([P, T], F32, name="placed")
         margin_sb = sb.tile([P, 1], F32, name="margin_sb")
         reserve_sb = sb.tile([P, 1], F32, name="reserve_sb")
-        neg_cap = sb.tile([P, 1], F32, name="neg_cap")
+        tiny = sb.tile([P, 1], F32, name="tiny")
 
         nc.vector.memset(k_bytes[:].bitcast(I32), 0)
+        nc.vector.memset(tiny[:], TINY)
         nc.vector.memset(v_bytes[:].bitcast(I32), 0)
-        nc.vector.memset(neg_cap[:], -CAP)
-        nc.vector.memset(placed[:], 0.0)
+        nc.vector.memset(placed[:, 0 : T // 2], 0.0)
+        nc.vector.memset(placed[:, T // 2 : T], 0.0)
 
         nc.sync.dma_start(offsets[:], offs)
         nc.sync.dma_start(q_raw[:], query.rearrange("(p j) w -> p j w", j=4))
@@ -55,18 +55,19 @@ def tile_attend_bsharedthreshold_s_kernel(tc, query, keys_words, keys_scales, ma
             nc.scalar.dma_start(k_bytes[32 * r : 32 * r + 4, :].bitcast(I32), keys_scales[0, 4 * r : 4 * r + 4, :].bitcast(I32))
         nc.sync.dma_start(k_words[:].bitcast(I32), keys_words[0].rearrange("p n t -> p (n t)").bitcast(I32))
         nc.sync.dma_start(g_raw[:], gout.rearrange("(p j) w -> p j w", j=4))
-        nc.sync.dma_start(v_words[:].bitcast(I32), vals_words[0].rearrange("p n t -> p (n t)").bitcast(I32))
-        nc.sync.dma_start(acc[:], old)
         nc.gpsimd.dma_start(margin_sb[:], margin)
         for r in range(4):
             nc.gpsimd.dma_start(v_bytes[32 * r + VPLANE : 32 * r + VPLANE + 4, :].bitcast(I32), vals_scales[0, 4 * r : 4 * r + 4, :].bitcast(I32))
         nc.gpsimd.dma_start(reserve_sb[:], reserve)
 
-        def quantise(raw, name):
+        warm = sb.tile([P, 1], F32, name="warm")
+        nc.scalar.activation(warm[:], tiny[:], ACT.Sigmoid, bias=tiny[:])
+
+        def quantise(raw, name, copy):
             grouped = sb.tile([P, Q, 4], BF16, name=name + "_grouped", align_bytes=64)
             codes = sb.tile([P, Q], U32, name=name + "_codes", align_bytes=64)
             scales = sb.tile([P, Q], U8, name=name + "_scales", align_bytes=64)
-            nc.scalar.copy(grouped[:], raw[:].rearrange("p j w -> p w j"))
+            copy(grouped[:], raw[:].rearrange("p j w -> p w j"))
             nc.vector.quantize_mx(codes[:].bitcast(FP8X4), scales[:], grouped[:].rearrange("p w j -> p (w j)"))
             return codes, scales
 
@@ -79,11 +80,9 @@ def tile_attend_bsharedthreshold_s_kernel(tc, query, keys_words, keys_scales, ma
         def spread(ap):
             return ap.unsqueeze(2).to_broadcast([P, HP, PAGE])
 
-        kg_bytes = sb.tile([P, I], U8, name="kg_bytes", align_bytes=64)
-        vg_bytes = sb.tile([P, I], U8, name="vg_bytes", align_bytes=64)
+        kg_bytes = sb.tile([P, I], U8, name="kg_bytes", tag="gathered_bytes", align_bytes=64)
         kg_words = sb.tile([P, I], U32, name="kg_words", align_bytes=64)
         vg_words = sb.tile([P, I], U32, name="vg_words", align_bytes=64)
-        margin_cap = sb.tile([P, 1], F32, name="margin_cap")
         a_ps = [ps.tile([P, HALF], F32, name="a_ps%d" % h) for h in range(2)]
         c_ps = ps.tile([P, I], F32, name="c_ps")
         a_sum = sb.tile([P, 2 * HP], F32, name="a_sum")
@@ -92,19 +91,22 @@ def tile_attend_bsharedthreshold_s_kernel(tc, query, keys_words, keys_scales, ma
         g = sb.tile([P, I], F32, name="g")
 
         nc.vector.tensor_copy(kg_bytes[:], k_bytes[:].indirect(offsets[:]))
-        q_codes, q_scales = quantise(q_raw, "q")
-        nc.vector.tensor_scalar_add(margin_cap[:], margin_sb[:], CAP)
+        q_codes, q_scales = quantise(q_raw, "q", nc.vector.tensor_copy)
+        v_words = sb.tile([P, T], U32, name="v_words", tag="q_then_v")
+        nc.sync.dma_start(v_words[:].bitcast(I32), vals_words[0].rearrange("p n t -> p (n t)").bitcast(I32))
         for h in range(2):
             nc.vector.tensor_copy(kg_words[:, halves[h]], k_words[:].indirect(offsets[:, pages[h]]))
             nc.tensor.matmul_mx(a_ps[h][:], lhsT=q_codes[:].bitcast(FP8X4), lhsT_scale=q_scales[:],
                                 rhs=kg_words[:, halves[h]].bitcast(FP8X4), rhs_scale=kg_bytes[:, halves[h]], start=True, stop=True)
-        g_codes, g_scales = quantise(g_raw, "g")
+        acc = sb.tile([P, T], F32, name="acc", tag="k_then_old")
+        nc.sync.dma_start(acc[:], old)
+        g_codes, g_scales = quantise(g_raw, "g", nc.scalar.copy)
         for h in range(2):
             nc.vector.tensor_reduce(a_sum[:, pages[h]], by_page(a_ps[h][:]), AX.X, ALU.add)
             nc.vector.scalar_tensor_tensor(by_page(w[:, halves[h]]), spread(a_sum[:, pages[h]]), 1.0 / PAGE, by_page(a_ps[h][:]), ALU.mult, ALU.subtract)
-            nc.scalar.activation(y[:, halves[h]], w[:, halves[h]], ACT.Relu, bias=margin_cap[:])
-            nc.scalar.activation(g[:, halves[h]], y[:, halves[h]], ACT.Sigmoid, bias=neg_cap[:])
+            nc.scalar.activation(g[:, halves[h]], w[:, halves[h]], ACT.Sigmoid, bias=margin_sb[:])
 
+        vg_bytes = sb.tile([P, I], U8, name="vg_bytes", tag="gathered_bytes", align_bytes=64)
         nc.vector.tensor_copy(vg_bytes[:], v_bytes[:].indirect(offsets[:]))
         nc.vector.tensor_copy(vg_words[:], v_words[:].indirect(offsets[:]))
         nc.tensor.matmul_mx(c_ps[:], lhsT=g_codes[:].bitcast(FP8X4), lhsT_scale=g_scales[:],
@@ -125,10 +127,10 @@ def tile_attend_bsharedthreshold_s_kernel(tc, query, keys_words, keys_scales, ma
         u_sum = sb.tile([P, 2 * HP], F32, name="u_sum")
 
         nc.vector.scalar_tensor_tensor(cs[:], g[:], 1.0, c_ps[:], ALU.subtract, ALU.mult)
+        for cols in (slice(0, LN_CUT), slice(LN_CUT, I)):
+            nc.scalar.activation(y[:, cols], g[:, cols], ACT.Ln, bias=tiny[:])
         for h in range(2):
-            nc.scalar.activation(y[:, halves[1 - h]], g[:, halves[h]], ACT.Ln)
-        for h in range(2):
-            nc.vector.scalar_tensor_tensor(pn[:, halves[h]], w[:, halves[h]], margin_sb[:], y[:, halves[1 - h]], ALU.add, ALU.min)
+            nc.vector.scalar_tensor_tensor(pn[:, halves[h]], w[:, halves[h]], margin_sb[:], y[:, halves[h]], ALU.add, ALU.min)
             nc.scalar.activation(sq[:, halves[h]], pn[:, halves[h]], ACT.Square, accum_out=s_part[h][:])
         nc.vector.scalar_tensor_tensor(cp[:], pn[:], 1.0, c_ps[:], ALU.mult, ALU.mult, accum_out=cp_sum[:])
         nc.vector.tensor_scalar(s_all[:], s_part[0][:], s_part[1][:], reserve_sb[:], ALU.add, ALU.add)

@@ -56,12 +56,12 @@ def tile_attend_bsharedthreshold_s_kernel(tc, query, keys_words, keys_scales, ma
         nc.sync.dma_start(k_words[:].bitcast(I32), keys_words[0].rearrange("p n t -> p (n t)").bitcast(I32))
         nc.sync.dma_start(g_raw[:], gout.rearrange("(p j) w -> p j w", j=4))
         nc.gpsimd.dma_start(margin_sb[:], margin)
-        for r in range(4):
-            nc.gpsimd.dma_start(v_bytes[32 * r + VPLANE : 32 * r + VPLANE + 4, :].bitcast(I32), vals_scales[0, 4 * r : 4 * r + 4, :].bitcast(I32))
         nc.gpsimd.dma_start(reserve_sb[:], reserve)
 
         warm = sb.tile([P, 1], F32, name="warm")
         nc.scalar.activation(warm[:], tiny[:], ACT.Sigmoid, bias=tiny[:])
+        for r in range(4):
+            nc.scalar.dma_start(v_bytes[32 * r + VPLANE : 32 * r + VPLANE + 4, :].bitcast(I32), vals_scales[0, 4 * r : 4 * r + 4, :].bitcast(I32))
 
         def quantise(raw, name, copy):
             grouped = sb.tile([P, Q, 4], BF16, name=name + "_grouped", align_bytes=64)
@@ -84,7 +84,7 @@ def tile_attend_bsharedthreshold_s_kernel(tc, query, keys_words, keys_scales, ma
         kg_words = sb.tile([P, I], U32, name="kg_words", align_bytes=64)
         vg_words = sb.tile([P, I], U32, name="vg_words", align_bytes=64)
         a_ps = [ps.tile([P, HALF], F32, name="a_ps%d" % h) for h in range(2)]
-        c_ps = ps.tile([P, I], F32, name="c_ps")
+        c_ps = [ps.tile([P, HALF], F32, name="c_ps%d" % h) for h in range(2)]
         a_sum = sb.tile([P, 2 * HP], F32, name="a_sum")
         w = sb.tile([P, I], F32, name="w")
         y = sb.tile([P, I], F32, name="y")
@@ -108,13 +108,13 @@ def tile_attend_bsharedthreshold_s_kernel(tc, query, keys_words, keys_scales, ma
 
         vg_bytes = sb.tile([P, I], U8, name="vg_bytes", tag="gathered_bytes", align_bytes=64)
         nc.vector.tensor_copy(vg_bytes[:], v_bytes[:].indirect(offsets[:]))
-        nc.vector.tensor_copy(vg_words[:], v_words[:].indirect(offsets[:]))
-        nc.tensor.matmul_mx(c_ps[:], lhsT=g_codes[:].bitcast(FP8X4), lhsT_scale=g_scales[:],
-                            rhs=vg_words[:].bitcast(FP8X4), rhs_scale=vg_bytes[VPLANE:P, :], start=True, stop=True)
+        for h in range(2):
+            nc.vector.tensor_copy(vg_words[:, halves[h]], v_words[:].indirect(offsets[:, pages[h]]))
+            nc.tensor.matmul_mx(c_ps[h][:], lhsT=g_codes[:].bitcast(FP8X4), lhsT_scale=g_scales[:],
+                                rhs=vg_words[:, halves[h]].bitcast(FP8X4), rhs_scale=vg_bytes[VPLANE:P, halves[h]], start=True, stop=True)
 
         pn = sb.tile([P, I], F32, name="pn")
         sq = sb.tile([P, I], F32, name="sq")
-        cs = sb.tile([P, I], F32, name="cs")
         pp = sb.tile([P, I], F32, name="pp")
         u = sb.tile([P, I], F32, name="u")
         cp = sb.tile([P, I], F32, name="cp")
@@ -122,24 +122,24 @@ def tile_attend_bsharedthreshold_s_kernel(tc, query, keys_words, keys_scales, ma
         s_part = [sb.tile([P, 1], F32, name="s_part%d" % h) for h in range(2)]
         s_all = sb.tile([P, 1], F32, name="s_all")
         rec = sb.tile([P, 1], F32, name="rec")
-        cp_sum = sb.tile([P, 1], F32, name="cp_sum")
+        cp_part = [sb.tile([P, 1], F32, name="cp_part%d" % h) for h in range(2)]
         kn = sb.tile([P, 1], F32, name="kn")
         u_sum = sb.tile([P, 2 * HP], F32, name="u_sum")
 
-        nc.vector.scalar_tensor_tensor(cs[:], g[:], 1.0, c_ps[:], ALU.subtract, ALU.mult)
         for cols in (slice(0, LN_CUT), slice(LN_CUT, I)):
             nc.scalar.activation(y[:, cols], g[:, cols], ACT.Ln, bias=tiny[:])
         for h in range(2):
             nc.vector.scalar_tensor_tensor(pn[:, halves[h]], w[:, halves[h]], margin_sb[:], y[:, halves[h]], ALU.add, ALU.min)
             nc.scalar.activation(sq[:, halves[h]], pn[:, halves[h]], ACT.Square, accum_out=s_part[h][:])
-        nc.vector.scalar_tensor_tensor(cp[:], pn[:], 1.0, c_ps[:], ALU.mult, ALU.mult, accum_out=cp_sum[:])
+        nc.vector.scalar_tensor_tensor(cp[:, halves[0]], pn[:, halves[0]], 1.0, c_ps[0][:], ALU.mult, ALU.mult, accum_out=cp_part[0][:])
         nc.vector.tensor_scalar(s_all[:], s_part[0][:], s_part[1][:], reserve_sb[:], ALU.add, ALU.add)
-        nc.vector.scalar_tensor_tensor(pp[:, halves[0]], g[:, halves[0]], 1.0, pn[:, halves[0]], ALU.subtract, ALU.mult)
+        nc.vector.scalar_tensor_tensor(cp[:, halves[1]], pn[:, halves[1]], 1.0, c_ps[1][:], ALU.mult, ALU.mult, accum_out=cp_part[1][:])
         nc.vector.reciprocal(rec[:], s_all[:])
-        nc.vector.scalar_tensor_tensor(pp[:, halves[1]], g[:, halves[1]], 1.0, pn[:, halves[1]], ALU.subtract, ALU.mult)
-        nc.vector.tensor_tensor(kn[:], cp_sum[:], rec[:], ALU.mult)
+        nc.vector.tensor_scalar(kn[:], cp_part[0][:], cp_part[1][:], rec[:], ALU.add, ALU.mult)
         for h in range(2):
-            nc.vector.scalar_tensor_tensor(u[:, halves[h]], pp[:, halves[h]], kn[:], cs[:, halves[h]], ALU.mult, ALU.subtract)
+            nc.vector.scalar_tensor_tensor(pp[:, halves[h]], pn[:, halves[h]], kn[:], c_ps[h][:], ALU.mult, ALU.subtract)
+        for h in range(2):
+            nc.vector.scalar_tensor_tensor(u[:, halves[h]], g[:, halves[h]], 1.0, pp[:, halves[h]], ALU.subtract, ALU.mult)
         for h in range(2):
             nc.vector.tensor_reduce(u_sum[:, pages[h]], by_page(u[:, halves[h]]), AX.X, ALU.add)
             nc.scalar.activation(by_page(mean[:, halves[h]]), spread(u_sum[:, pages[h]]), ACT.Copy, scale=-1.0 / PAGE)

@@ -1,3 +1,4 @@
+import math
 from contextlib import ExitStack
 
 import concourse.mybir as mybir
@@ -17,137 +18,148 @@ ACT = mybir.ActivationFunctionType
 AX = mybir.AxisListType
 
 P = 128
+PACK = 4
 PAGE = 16
 HALF = I // 2
-HP = HALF // PAGE
-TINY = 2.0**-60
+HALF_PAGES = HALF // PAGE
+GRAD_FACTOR = 16.0
+FLOOR_AT = 60.0 * math.log(2.0)
+V_ROW = 4
 LN_CUT = HALF + 2 * PAGE
-VPLANE = 4
 OUT_CUTS = (0, 256, 768, 1280, 1792, 2048)
 
 
 def tile_attend_bsharedthreshold_s_kernel(tc, query, keys_words, keys_scales, margin, reserve, gout, vals_words, vals_scales, old, offs, out):
     nc = tc.nc
+    halves = [slice(h * HALF, (h + 1) * HALF) for h in range(2)]
+    pages = [slice(h * HALF_PAGES, (h + 1) * HALF_PAGES) for h in range(2)]
+
+    def by_page(ap):
+        return ap.rearrange("p (g i) -> p g i", i=PAGE)
+
+    def spread(ap):
+        return ap.unsqueeze(2).to_broadcast([P, HALF_PAGES, PAGE])
+
+    def load_scale_rows(tile, scales, first_row):
+        for quad in range(4):
+            rows = slice(32 * quad + first_row, 32 * quad + first_row + 4)
+            nc.sync.dma_start(tile[rows, :].bitcast(I32), scales[0, 4 * quad : 4 * quad + 4, :].bitcast(I32))
+
+    def load_words(tile, words):
+        nc.sync.dma_start(tile[:].bitcast(I32), words[0].rearrange("p n t -> p (n t)").bitcast(I32))
+
     with ExitStack() as ctx:
         sb = ctx.enter_context(tc.tile_pool(name="sb", bufs=1))
         ps = ctx.enter_context(tc.psum_pool(name="ps", bufs=1))
 
-        offsets = sb.tile([P, I // 16], U16, name="offsets")
+        def quantise(raw, name, copy, grouped_tag):
+            grouped = sb.tile([P, Q, PACK], BF16, name=name + "_grouped", tag=grouped_tag, align_bytes=64)
+            codes = sb.tile([P, Q], U32, name=name + "_codes", align_bytes=64)
+            scales = sb.tile([P, Q], U8, name=name + "_scales", align_bytes=64)
+            copy(grouped[:], raw[:].rearrange("p t w -> p w t"))
+            nc.vector.quantize_mx(codes[:].bitcast(FP8X4), scales[:], grouped[:].rearrange("p w t -> p (w t)"))
+            return codes, scales
+
+        offsets = sb.tile([P, I // PAGE], U16, name="offsets")
         k_bytes = sb.tile([P, T], U8, name="k_bytes")
         v_bytes = sb.tile([P, T], U8, name="v_bytes")
-        k_words = sb.tile([P, T], U32, name="k_words", tag="k_then_old")
-        q_raw = sb.tile([P, 4, Q], F32, name="q_raw", tag="q_then_v")
-        g_raw = sb.tile([P, 4, Q], F32, name="g_raw")
+        one = sb.tile([P, 1], F32, name="one", tag="one_keys_old")
+        q_raw = sb.tile([P, PACK, Q], F32, name="q_raw", tag="query_gout_sig")
         placed = sb.tile([P, T], F32, name="placed")
         margin_sb = sb.tile([P, 1], F32, name="margin_sb")
         reserve_sb = sb.tile([P, 1], F32, name="reserve_sb")
-        tiny = sb.tile([P, 1], F32, name="tiny")
+        floor_arg = sb.tile([P, 1], F32, name="floor_arg")
+        floor = sb.tile([P, 1], F32, name="floor")
 
         nc.vector.memset(k_bytes[:].bitcast(I32), 0)
-        nc.vector.memset(tiny[:], TINY)
+        nc.vector.memset(one[:], 1.0)
+        nc.vector.tensor_scalar_mul(floor_arg[:], one[:], -FLOOR_AT)
         nc.vector.memset(v_bytes[:].bitcast(I32), 0)
         nc.vector.memset(placed[:, 0 : T // 2], 0.0)
         nc.vector.memset(placed[:, T // 2 : T], 0.0)
 
         nc.sync.dma_start(offsets[:], offs)
-        nc.sync.dma_start(q_raw[:], query.rearrange("(p j) w -> p j w", j=4))
-        for r in range(4):
-            nc.scalar.dma_start(k_bytes[32 * r : 32 * r + 4, :].bitcast(I32), keys_scales[0, 4 * r : 4 * r + 4, :].bitcast(I32))
-        nc.sync.dma_start(k_words[:].bitcast(I32), keys_words[0].rearrange("p n t -> p (n t)").bitcast(I32))
-        nc.sync.dma_start(g_raw[:], gout.rearrange("(p j) w -> p j w", j=4))
+        nc.sync.dma_start(q_raw[:], query.rearrange("(p t) w -> p t w", t=PACK))
+        load_scale_rows(k_bytes, keys_scales, 0)
+        k_words = sb.tile([P, T], U32, name="k_words", tag="one_keys_old")
+        load_words(k_words, keys_words)
         nc.gpsimd.dma_start(margin_sb[:], margin)
         nc.gpsimd.dma_start(reserve_sb[:], reserve)
-
-        warm = sb.tile([P, 1], F32, name="warm")
-        nc.scalar.activation(warm[:], tiny[:], ACT.Sigmoid, bias=tiny[:])
-        for r in range(4):
-            nc.scalar.dma_start(v_bytes[32 * r + VPLANE : 32 * r + VPLANE + 4, :].bitcast(I32), vals_scales[0, 4 * r : 4 * r + 4, :].bitcast(I32))
-
-        def quantise(raw, name, copy):
-            grouped = sb.tile([P, Q, 4], BF16, name=name + "_grouped", align_bytes=64)
-            codes = sb.tile([P, Q], U32, name=name + "_codes", align_bytes=64)
-            scales = sb.tile([P, Q], U8, name=name + "_scales", align_bytes=64)
-            copy(grouped[:], raw[:].rearrange("p j w -> p w j"))
-            nc.vector.quantize_mx(codes[:].bitcast(FP8X4), scales[:], grouped[:].rearrange("p w j -> p (w j)"))
-            return codes, scales
-
-        halves = [slice(h * HALF, (h + 1) * HALF) for h in range(2)]
-        pages = [slice(h * HP, (h + 1) * HP) for h in range(2)]
-
-        def by_page(ap):
-            return ap.rearrange("p (g i) -> p g i", i=PAGE)
-
-        def spread(ap):
-            return ap.unsqueeze(2).to_broadcast([P, HP, PAGE])
+        nc.scalar.activation(floor[:], floor_arg[:], ACT.Sigmoid)
+        load_scale_rows(v_bytes, vals_scales, V_ROW)
 
         kg_bytes = sb.tile([P, I], U8, name="kg_bytes", tag="gathered_bytes", align_bytes=64)
         kg_words = sb.tile([P, I], U32, name="kg_words", align_bytes=64)
-        vg_words = sb.tile([P, I], U32, name="vg_words", align_bytes=64)
         a_ps = [ps.tile([P, HALF], F32, name="a_ps%d" % h) for h in range(2)]
-        c_ps = [ps.tile([P, HALF], F32, name="c_ps%d" % h) for h in range(2)]
-        a_sum = sb.tile([P, 2 * HP], F32, name="a_sum")
-        w = sb.tile([P, I], F32, name="w")
-        y = sb.tile([P, I], F32, name="y")
-        g = sb.tile([P, I], F32, name="g")
-
+        q_codes, q_scales = quantise(q_raw, "q", nc.vector.tensor_copy, "grouped_vals")
         nc.vector.tensor_copy(kg_bytes[:], k_bytes[:].indirect(offsets[:]))
-        q_codes, q_scales = quantise(q_raw, "q", nc.vector.tensor_copy)
-        v_words = sb.tile([P, T], U32, name="v_words", tag="q_then_v")
-        nc.sync.dma_start(v_words[:].bitcast(I32), vals_words[0].rearrange("p n t -> p (n t)").bitcast(I32))
+        g_raw = sb.tile([P, PACK, Q], F32, name="g_raw", tag="query_gout_sig")
+        nc.sync.dma_start(g_raw[:], gout.rearrange("(p t) w -> p t w", t=PACK))
+        v_words = sb.tile([P, T], U32, name="v_words", tag="grouped_vals", align_bytes=64)
+        load_words(v_words, vals_words)
         for h in range(2):
             nc.vector.tensor_copy(kg_words[:, halves[h]], k_words[:].indirect(offsets[:, pages[h]]))
+        for h in range(2):
             nc.tensor.matmul_mx(a_ps[h][:], lhsT=q_codes[:].bitcast(FP8X4), lhsT_scale=q_scales[:],
                                 rhs=kg_words[:, halves[h]].bitcast(FP8X4), rhs_scale=kg_bytes[:, halves[h]], start=True, stop=True)
-        acc = sb.tile([P, T], F32, name="acc", tag="k_then_old")
-        nc.sync.dma_start(acc[:], old)
-        g_codes, g_scales = quantise(g_raw, "g", nc.scalar.copy)
+        total = sb.tile([P, T], F32, name="total", tag="one_keys_old")
+        nc.sync.dma_start(total[:], old)
+        g_codes, g_scales = quantise(g_raw, "g", nc.scalar.copy, "g_grouped")
+
+        a_sum = sb.tile([P, I // PAGE], F32, name="a_sum")
+        below = sb.tile([P, I], F32, name="below")
+        sig_neg = sb.tile([P, I], F32, name="sig_neg", tag="query_gout_sig")
         for h in range(2):
             nc.vector.tensor_reduce(a_sum[:, pages[h]], by_page(a_ps[h][:]), AX.X, ALU.add)
-            nc.vector.scalar_tensor_tensor(by_page(w[:, halves[h]]), spread(a_sum[:, pages[h]]), 1.0 / PAGE, by_page(a_ps[h][:]), ALU.mult, ALU.subtract)
-            nc.scalar.activation(g[:, halves[h]], w[:, halves[h]], ACT.Sigmoid, bias=margin_sb[:])
+            nc.vector.scalar_tensor_tensor(by_page(below[:, halves[h]]), spread(a_sum[:, pages[h]]), 1.0 / PAGE, by_page(a_ps[h][:]), ALU.mult, ALU.subtract)
+            nc.scalar.activation(sig_neg[:, halves[h]], below[:, halves[h]], ACT.Sigmoid, bias=margin_sb[:])
 
         vg_bytes = sb.tile([P, I], U8, name="vg_bytes", tag="gathered_bytes", align_bytes=64)
+        vg_words = sb.tile([P, I], U32, name="vg_words", align_bytes=64)
+        c_ps = [ps.tile([P, HALF], F32, name="c_ps%d" % h) for h in range(2)]
         nc.vector.tensor_copy(vg_bytes[:], v_bytes[:].indirect(offsets[:]))
         for h in range(2):
             nc.vector.tensor_copy(vg_words[:, halves[h]], v_words[:].indirect(offsets[:, pages[h]]))
             nc.tensor.matmul_mx(c_ps[h][:], lhsT=g_codes[:].bitcast(FP8X4), lhsT_scale=g_scales[:],
-                                rhs=vg_words[:, halves[h]].bitcast(FP8X4), rhs_scale=vg_bytes[VPLANE:P, halves[h]], start=True, stop=True)
+                                rhs=vg_words[:, halves[h]].bitcast(FP8X4), rhs_scale=vg_bytes[V_ROW:P, halves[h]], start=True, stop=True)
 
-        pn = sb.tile([P, I], F32, name="pn")
-        sq = sb.tile([P, I], F32, name="sq")
-        pp = sb.tile([P, I], F32, name="pp")
-        u = sb.tile([P, I], F32, name="u")
-        cp = sb.tile([P, I], F32, name="cp")
-        mean = sb.tile([P, I], F32, name="mean")
-        s_part = [sb.tile([P, 1], F32, name="s_part%d" % h) for h in range(2)]
-        s_all = sb.tile([P, 1], F32, name="s_all")
-        rec = sb.tile([P, 1], F32, name="rec")
-        cp_part = [sb.tile([P, 1], F32, name="cp_part%d" % h) for h in range(2)]
-        kn = sb.tile([P, 1], F32, name="kn")
-        u_sum = sb.tile([P, 2 * HP], F32, name="u_sum")
-
+        log_sig = sb.tile([P, I], F32, name="log_sig")
+        p_neg = sb.tile([P, I], F32, name="p_neg")
+        p_square = sb.tile([P, I], F32, name="p_square")
+        cp_neg = sb.tile([P, I], F32, name="cp_neg")
+        square_sum = [sb.tile([P, 1], F32, name="square_sum%d" % h) for h in range(2)]
+        cp_neg_sum = [sb.tile([P, 1], F32, name="cp_neg_sum%d" % h) for h in range(2)]
+        s_row = sb.tile([P, 1], F32, name="s_row")
+        s_inverse = sb.tile([P, 1], F32, name="s_inverse")
+        ratio_neg = sb.tile([P, 1], F32, name="ratio_neg")
         for cols in (slice(0, LN_CUT), slice(LN_CUT, I)):
-            nc.scalar.activation(y[:, cols], g[:, cols], ACT.Ln, bias=tiny[:])
+            nc.scalar.activation(log_sig[:, cols], sig_neg[:, cols], ACT.Ln, bias=floor[:])
         for h in range(2):
-            nc.vector.scalar_tensor_tensor(pn[:, halves[h]], w[:, halves[h]], margin_sb[:], y[:, halves[h]], ALU.add, ALU.min)
-            nc.scalar.activation(sq[:, halves[h]], pn[:, halves[h]], ACT.Square, accum_out=s_part[h][:])
-        nc.vector.scalar_tensor_tensor(cp[:, halves[0]], pn[:, halves[0]], 1.0, c_ps[0][:], ALU.mult, ALU.mult, accum_out=cp_part[0][:])
-        nc.vector.tensor_scalar(s_all[:], s_part[0][:], s_part[1][:], reserve_sb[:], ALU.add, ALU.add)
-        nc.vector.scalar_tensor_tensor(cp[:, halves[1]], pn[:, halves[1]], 1.0, c_ps[1][:], ALU.mult, ALU.mult, accum_out=cp_part[1][:])
-        nc.vector.reciprocal(rec[:], s_all[:])
-        nc.vector.tensor_scalar(kn[:], cp_part[0][:], cp_part[1][:], rec[:], ALU.add, ALU.mult)
+            nc.vector.scalar_tensor_tensor(p_neg[:, halves[h]], below[:, halves[h]], margin_sb[:], log_sig[:, halves[h]], ALU.add, ALU.min)
+            nc.scalar.activation(p_square[:, halves[h]], p_neg[:, halves[h]], ACT.Square, accum_out=square_sum[h][:])
+        nc.vector.scalar_tensor_tensor(cp_neg[:, halves[0]], p_neg[:, halves[0]], 1.0, c_ps[0][:], ALU.mult, ALU.mult, accum_out=cp_neg_sum[0][:])
+        nc.vector.tensor_scalar(s_row[:], square_sum[0][:], square_sum[1][:], reserve_sb[:], ALU.add, ALU.add)
+        nc.vector.scalar_tensor_tensor(cp_neg[:, halves[1]], p_neg[:, halves[1]], 1.0, c_ps[1][:], ALU.mult, ALU.mult, accum_out=cp_neg_sum[1][:])
+        nc.vector.reciprocal(s_inverse[:], s_row[:])
+        nc.vector.tensor_scalar(ratio_neg[:], cp_neg_sum[0][:], cp_neg_sum[1][:], s_inverse[:], ALU.add, ALU.mult)
+
+        v_neg = sb.tile([P, I], F32, name="v_neg")
+        u = sb.tile([P, I], F32, name="u")
+        u_sum = sb.tile([P, I // PAGE], F32, name="u_sum")
+        u_mean_neg = sb.tile([P, I], F32, name="u_mean_neg")
         for h in range(2):
-            nc.vector.scalar_tensor_tensor(pp[:, halves[h]], pn[:, halves[h]], kn[:], c_ps[h][:], ALU.mult, ALU.subtract)
+            nc.vector.scalar_tensor_tensor(v_neg[:, halves[h]], p_neg[:, halves[h]], ratio_neg[:], c_ps[h][:], ALU.mult, ALU.subtract)
         for h in range(2):
-            nc.vector.scalar_tensor_tensor(u[:, halves[h]], g[:, halves[h]], 1.0, pp[:, halves[h]], ALU.subtract, ALU.mult)
+            nc.vector.scalar_tensor_tensor(u[:, halves[h]], sig_neg[:, halves[h]], 1.0, v_neg[:, halves[h]], ALU.subtract, ALU.mult)
         for h in range(2):
             nc.vector.tensor_reduce(u_sum[:, pages[h]], by_page(u[:, halves[h]]), AX.X, ALU.add)
-            nc.scalar.activation(by_page(mean[:, halves[h]]), spread(u_sum[:, pages[h]]), ACT.Copy, scale=-1.0 / PAGE)
-        alpha = u_sum[:, 2 * HP - 1 : 2 * HP]
-        nc.scalar.activation(alpha, rec[:], ACT.Sqrt, scale=256.0)
+            nc.scalar.activation(by_page(u_mean_neg[:, halves[h]]), spread(u_sum[:, pages[h]]), ACT.Copy, scale=-1.0 / PAGE)
+
+        row_factor = u_sum[:, I // PAGE - 1 : I // PAGE]
+        nc.scalar.activation(row_factor, s_inverse[:], ACT.Sqrt, scale=GRAD_FACTOR * GRAD_FACTOR)
         for h in range(2):
-            nc.vector.tensor_tensor(placed[:].indirect(offsets[:, pages[h]]), u[:, halves[h]], mean[:, halves[h]], ALU.add)
+            nc.vector.tensor_tensor(placed[:].indirect(offsets[:, pages[h]]), u[:, halves[h]], u_mean_neg[:, halves[h]], ALU.add)
         for c in range(len(OUT_CUTS) - 1):
             cols = slice(OUT_CUTS[c], OUT_CUTS[c + 1])
-            nc.vector.scalar_tensor_tensor(acc[:, cols], placed[:, cols], alpha, acc[:, cols], ALU.mult, ALU.add)
-            nc.sync.dma_start(out[:, cols], acc[:, cols])
+            nc.vector.scalar_tensor_tensor(total[:, cols], placed[:, cols], row_factor, total[:, cols], ALU.mult, ALU.add)
+            nc.sync.dma_start(out[:, cols], total[:, cols])

@@ -52,11 +52,14 @@ def tile_attend_bsharedthreshold_s_kernel(tc, query, keys_words, keys_scales, ma
         sb = ctx.enter_context(tc.tile_pool(name="sb", bufs=1))
         ps = ctx.enter_context(tc.psum_pool(name="ps", bufs=1))
 
-        def quantise(raw, name, copy, grouped_tag):
-            grouped = sb.tile([P, Q, PACK], BF16, name=name + "_grouped", tag=grouped_tag, align_bytes=64)
+        def group(raw, name, tag):
+            grouped = sb.tile([P, Q, PACK], BF16, name=name, tag=tag, align_bytes=64)
+            nc.scalar.copy(grouped[:], raw[:].rearrange("p t w -> p w t"))
+            return grouped
+
+        def quantise(grouped, name, scales_tag):
             codes = sb.tile([P, Q], U32, name=name + "_codes", align_bytes=64)
-            scales = sb.tile([P, Q], U8, name=name + "_scales", align_bytes=64)
-            copy(grouped[:], raw[:].rearrange("p t w -> p w t"))
+            scales = sb.tile([P, Q], U8, name=name + "_scales", tag=scales_tag, align_bytes=64)
             nc.vector.quantize_mx(codes[:].bitcast(FP8X4), scales[:], grouped[:].rearrange("p w t -> p (w t)"))
             return codes, scales
 
@@ -66,13 +69,11 @@ def tile_attend_bsharedthreshold_s_kernel(tc, query, keys_words, keys_scales, ma
         one = sb.tile([P, 1], F32, name="one", tag="one_keys_old")
         q_raw = sb.tile([P, PACK, Q], F32, name="q_raw", tag="query_gout_sig")
         placed = sb.tile([P, T], F32, name="placed")
-        margin_sb = sb.tile([P, 1], F32, name="margin_sb")
-        reserve_sb = sb.tile([P, 1], F32, name="reserve_sb")
-        floor_arg = sb.tile([P, 1], F32, name="floor_arg")
+        floor_arg = sb.tile([P, 1], F32, name="floor_arg", tag="floor_margin")
         floor = sb.tile([P, 1], F32, name="floor")
 
-        nc.vector.memset(k_bytes[:].bitcast(I32), 0)
         nc.vector.memset(one[:], 1.0)
+        nc.vector.memset(k_bytes[:].bitcast(I32), 0)
         nc.vector.tensor_scalar_mul(floor_arg[:], one[:], -FLOOR_AT)
         nc.vector.memset(v_bytes[:].bitcast(I32), 0)
         nc.vector.memset(placed[:, 0 : T // 2], 0.0)
@@ -83,16 +84,17 @@ def tile_attend_bsharedthreshold_s_kernel(tc, query, keys_words, keys_scales, ma
         load_scale_rows(k_bytes, keys_scales, 0)
         k_words = sb.tile([P, T], U32, name="k_words", tag="one_keys_old")
         load_words(k_words, keys_words)
-        nc.gpsimd.dma_start(margin_sb[:], margin)
-        nc.gpsimd.dma_start(reserve_sb[:], reserve)
         nc.scalar.activation(floor[:], floor_arg[:], ACT.Sigmoid)
         load_scale_rows(v_bytes, vals_scales, V_ROW)
+        margin_sb = sb.tile([P, 1], F32, name="margin_sb", tag="floor_margin")
+        nc.sync.dma_start(margin_sb[:], margin)
 
         kg_bytes = sb.tile([P, I], U8, name="kg_bytes", tag="gathered_bytes", align_bytes=64)
         kg_words = sb.tile([P, I], U32, name="kg_words", align_bytes=64)
         a_ps = [ps.tile([P, HALF], F32, name="a_ps%d" % h) for h in range(2)]
-        q_codes, q_scales = quantise(q_raw, "q", nc.vector.tensor_copy, "grouped_vals")
+        q_grouped = group(q_raw, "q_grouped", "grouped_vals")
         nc.vector.tensor_copy(kg_bytes[:], k_bytes[:].indirect(offsets[:]))
+        q_codes, q_scales = quantise(q_grouped, "q", "scales_reserve")
         g_raw = sb.tile([P, PACK, Q], F32, name="g_raw", tag="query_gout_sig")
         nc.sync.dma_start(g_raw[:], gout.rearrange("(p t) w -> p t w", t=PACK))
         v_words = sb.tile([P, T], U32, name="v_words", tag="grouped_vals", align_bytes=64)
@@ -104,7 +106,9 @@ def tile_attend_bsharedthreshold_s_kernel(tc, query, keys_words, keys_scales, ma
                                 rhs=kg_words[:, halves[h]].bitcast(FP8X4), rhs_scale=kg_bytes[:, halves[h]], start=True, stop=True)
         total = sb.tile([P, T], F32, name="total", tag="one_keys_old")
         nc.sync.dma_start(total[:], old)
-        g_codes, g_scales = quantise(g_raw, "g", nc.scalar.copy, "g_grouped")
+        reserve_sb = sb.tile([P, 1], F32, name="reserve_sb", tag="scales_reserve", align_bytes=64)
+        nc.sync.dma_start(reserve_sb[:], reserve)
+        g_grouped = group(g_raw, "g_grouped", "g_grouped")
 
         a_sum = sb.tile([P, I // PAGE], F32, name="a_sum")
         below = sb.tile([P, I], F32, name="below")
@@ -117,6 +121,7 @@ def tile_attend_bsharedthreshold_s_kernel(tc, query, keys_words, keys_scales, ma
         vg_bytes = sb.tile([P, I], U8, name="vg_bytes", tag="gathered_bytes", align_bytes=64)
         vg_words = sb.tile([P, I], U32, name="vg_words", align_bytes=64)
         c_ps = [ps.tile([P, HALF], F32, name="c_ps%d" % h) for h in range(2)]
+        g_codes, g_scales = quantise(g_grouped, "g", "g_scales")
         nc.vector.tensor_copy(vg_bytes[:], v_bytes[:].indirect(offsets[:]))
         for h in range(2):
             nc.vector.tensor_copy(vg_words[:, halves[h]], v_words[:].indirect(offsets[:, pages[h]]))

import math
from contextlib import ExitStack

import concourse.mybir as mybir

D, T, I, Q = 512, 2048, 512, 128
FLOPS = 2 * 2 * D * Q * I

F32 = mybir.dt.float32
BF16 = mybir.dt.bfloat16
I32 = mybir.dt.int32
U32 = mybir.dt.uint32
U16 = mybir.dt.uint16
U8 = mybir.dt.uint8
FP8X4 = mybir.dt.float8_e4m3fn_x4
ALU = mybir.AluOpType
ACT = mybir.ActivationFunctionType
AX = mybir.AxisListType

P = 128
PACK = 4
PAGE = 16
HALF = I // 2
HALF_PAGES = HALF // PAGE
GRAD_FACTOR = 16.0
FLOOR_AT = 60.0 * math.log(2.0)
V_ROW = 4
LN_CUT = HALF + 2 * PAGE
OUT_CUTS = (0, 256, 768, 1280, 1792, 2048)


def tile_attend_bsharedthreshold_s_kernel(tc, query, keys_words, keys_scales, margin, reserve, gout, vals_words, vals_scales, old, offs, out):
    nc = tc.nc
    halves = [slice(h * HALF, (h + 1) * HALF) for h in range(2)]
    pages = [slice(h * HALF_PAGES, (h + 1) * HALF_PAGES) for h in range(2)]

    def by_page(ap):
        return ap.rearrange("p (g i) -> p g i", i=PAGE)

    def spread(ap):
        return ap.unsqueeze(2).to_broadcast([P, HALF_PAGES, PAGE])

    def load_scale_rows(tile, scales, first_row):
        for quad in range(4):
            rows = slice(32 * quad + first_row, 32 * quad + first_row + 4)
            nc.sync.dma_start(tile[rows, :].bitcast(I32), scales[0, 4 * quad : 4 * quad + 4, :].bitcast(I32))

    def load_words(tile, words):
        nc.sync.dma_start(tile[:].bitcast(I32), words[0].rearrange("p n t -> p (n t)").bitcast(I32))

    with ExitStack() as ctx:
        sb = ctx.enter_context(tc.tile_pool(name="sb", bufs=1))
        ps = ctx.enter_context(tc.psum_pool(name="ps", bufs=1))

        def group(raw, name, tag):
            grouped = sb.tile([P, Q, PACK], BF16, name=name, tag=tag, align_bytes=64)
            nc.scalar.copy(grouped[:], raw[:].rearrange("p t w -> p w t"))
            return grouped

        def quantise(grouped, name, scales_tag):
            codes = sb.tile([P, Q], U32, name=name + "_codes", align_bytes=64)
            scales = sb.tile([P, Q], U8, name=name + "_scales", tag=scales_tag, align_bytes=64)
            nc.vector.quantize_mx(codes[:].bitcast(FP8X4), scales[:], grouped[:].rearrange("p w t -> p (w t)"))
            return codes, scales

        offsets = sb.tile([P, I // PAGE], U16, name="offsets")
        k_bytes = sb.tile([P, T], U8, name="k_bytes")
        v_bytes = sb.tile([P, T], U8, name="v_bytes")
        one = sb.tile([P, 1], F32, name="one", tag="one_keys_old")
        q_raw = sb.tile([P, PACK, Q], F32, name="q_raw", tag="query_gout_sig")
        placed = sb.tile([P, T], F32, name="placed")
        floor_arg = sb.tile([P, 1], F32, name="floor_arg", tag="floor_margin")
        floor = sb.tile([P, 1], F32, name="floor")

        nc.vector.memset(one[:], 1.0)
        nc.vector.memset(k_bytes[:].bitcast(I32), 0)
        nc.vector.tensor_scalar_mul(floor_arg[:], one[:], -FLOOR_AT)
        nc.vector.memset(v_bytes[:].bitcast(I32), 0)
        nc.vector.memset(placed[:, 0 : T // 2], 0.0)
        nc.vector.memset(placed[:, T // 2 : T], 0.0)

        nc.sync.dma_start(offsets[:], offs)
        nc.sync.dma_start(q_raw[:], query.rearrange("(p t) w -> p t w", t=PACK))
        load_scale_rows(k_bytes, keys_scales, 0)
        k_words = sb.tile([P, T], U32, name="k_words", tag="one_keys_old")
        load_words(k_words, keys_words)
        nc.scalar.activation(floor[:], floor_arg[:], ACT.Sigmoid)
        load_scale_rows(v_bytes, vals_scales, V_ROW)
        margin_sb = sb.tile([P, 1], F32, name="margin_sb", tag="floor_margin")
        nc.sync.dma_start(margin_sb[:], margin)

        kg_bytes = sb.tile([P, I], U8, name="kg_bytes", tag="gathered_bytes", align_bytes=64)
        kg_words = sb.tile([P, I], U32, name="kg_words", align_bytes=64)
        a_ps = [ps.tile([P, HALF], F32, name="a_ps%d" % h) for h in range(2)]
        q_grouped = group(q_raw, "q_grouped", "grouped_vals")
        nc.vector.tensor_copy(kg_bytes[:], k_bytes[:].indirect(offsets[:]))
        q_codes, q_scales = quantise(q_grouped, "q", "scales_reserve")
        g_raw = sb.tile([P, PACK, Q], F32, name="g_raw", tag="query_gout_sig")
        nc.sync.dma_start(g_raw[:], gout.rearrange("(p t) w -> p t w", t=PACK))
        v_words = sb.tile([P, T], U32, name="v_words", tag="grouped_vals", align_bytes=64)
        load_words(v_words, vals_words)
        for h in range(2):
            nc.vector.tensor_copy(kg_words[:, halves[h]], k_words[:].indirect(offsets[:, pages[h]]))
        for h in range(2):
            nc.tensor.matmul_mx(a_ps[h][:], lhsT=q_codes[:].bitcast(FP8X4), lhsT_scale=q_scales[:],
                                rhs=kg_words[:, halves[h]].bitcast(FP8X4), rhs_scale=kg_bytes[:, halves[h]], start=True, stop=True)
        total = sb.tile([P, T], F32, name="total", tag="one_keys_old")
        nc.sync.dma_start(total[:], old)
        reserve_sb = sb.tile([P, 1], F32, name="reserve_sb", tag="scales_reserve", align_bytes=64)
        nc.sync.dma_start(reserve_sb[:], reserve)
        g_grouped = group(g_raw, "g_grouped", "g_grouped")

        a_sum = sb.tile([P, I // PAGE], F32, name="a_sum")
        below = sb.tile([P, I], F32, name="below")
        sig_neg = sb.tile([P, I], F32, name="sig_neg", tag="query_gout_sig")
        for h in range(2):
            nc.vector.tensor_reduce(a_sum[:, pages[h]], by_page(a_ps[h][:]), AX.X, ALU.add)
            nc.vector.scalar_tensor_tensor(by_page(below[:, halves[h]]), spread(a_sum[:, pages[h]]), 1.0 / PAGE, by_page(a_ps[h][:]), ALU.mult, ALU.subtract)
            nc.scalar.activation(sig_neg[:, halves[h]], below[:, halves[h]], ACT.Sigmoid, bias=margin_sb[:])

        vg_bytes = sb.tile([P, I], U8, name="vg_bytes", tag="gathered_bytes", align_bytes=64)
        vg_words = sb.tile([P, I], U32, name="vg_words", align_bytes=64)
        c_ps = [ps.tile([P, HALF], F32, name="c_ps%d" % h) for h in range(2)]
        g_codes, g_scales = quantise(g_grouped, "g", "g_scales")
        nc.vector.tensor_copy(vg_bytes[:], v_bytes[:].indirect(offsets[:]))
        for h in range(2):
            nc.vector.tensor_copy(vg_words[:, halves[h]], v_words[:].indirect(offsets[:, pages[h]]))
            nc.tensor.matmul_mx(c_ps[h][:], lhsT=g_codes[:].bitcast(FP8X4), lhsT_scale=g_scales[:],
                                rhs=vg_words[:, halves[h]].bitcast(FP8X4), rhs_scale=vg_bytes[V_ROW:P, halves[h]], start=True, stop=True)

        log_sig = sb.tile([P, I], F32, name="log_sig")
        p_neg = sb.tile([P, I], F32, name="p_neg")
        p_square = sb.tile([P, I], F32, name="p_square")
        cp_neg = sb.tile([P, I], F32, name="cp_neg")
        square_sum = [sb.tile([P, 1], F32, name="square_sum%d" % h) for h in range(2)]
        cp_neg_sum = [sb.tile([P, 1], F32, name="cp_neg_sum%d" % h) for h in range(2)]
        s_row = sb.tile([P, 1], F32, name="s_row")
        s_inverse = sb.tile([P, 1], F32, name="s_inverse")
        ratio_neg = sb.tile([P, 1], F32, name="ratio_neg")
        for cols in (slice(0, LN_CUT), slice(LN_CUT, I)):
            nc.scalar.activation(log_sig[:, cols], sig_neg[:, cols], ACT.Ln, bias=floor[:])
        for h in range(2):
            nc.vector.scalar_tensor_tensor(p_neg[:, halves[h]], below[:, halves[h]], margin_sb[:], log_sig[:, halves[h]], ALU.add, ALU.min)
            nc.scalar.activation(p_square[:, halves[h]], p_neg[:, halves[h]], ACT.Square, accum_out=square_sum[h][:])
        nc.vector.scalar_tensor_tensor(cp_neg[:, halves[0]], p_neg[:, halves[0]], 1.0, c_ps[0][:], ALU.mult, ALU.mult, accum_out=cp_neg_sum[0][:])
        nc.vector.tensor_scalar(s_row[:], square_sum[0][:], square_sum[1][:], reserve_sb[:], ALU.add, ALU.add)
        nc.vector.scalar_tensor_tensor(cp_neg[:, halves[1]], p_neg[:, halves[1]], 1.0, c_ps[1][:], ALU.mult, ALU.mult, accum_out=cp_neg_sum[1][:])
        nc.vector.reciprocal(s_inverse[:], s_row[:])
        nc.vector.tensor_scalar(ratio_neg[:], cp_neg_sum[0][:], cp_neg_sum[1][:], s_inverse[:], ALU.add, ALU.mult)

        v_neg = sb.tile([P, I], F32, name="v_neg")
        u = sb.tile([P, I], F32, name="u")
        u_sum = sb.tile([P, I // PAGE], F32, name="u_sum")
        u_mean_neg = sb.tile([P, I], F32, name="u_mean_neg")
        for h in range(2):
            nc.vector.scalar_tensor_tensor(v_neg[:, halves[h]], p_neg[:, halves[h]], ratio_neg[:], c_ps[h][:], ALU.mult, ALU.subtract)
        for h in range(2):
            nc.vector.scalar_tensor_tensor(u[:, halves[h]], sig_neg[:, halves[h]], 1.0, v_neg[:, halves[h]], ALU.subtract, ALU.mult)
        for h in range(2):
            nc.vector.tensor_reduce(u_sum[:, pages[h]], by_page(u[:, halves[h]]), AX.X, ALU.add)
            nc.scalar.activation(by_page(u_mean_neg[:, halves[h]]), spread(u_sum[:, pages[h]]), ACT.Copy, scale=-1.0 / PAGE)

        row_factor = u_sum[:, I // PAGE - 1 : I // PAGE]
        nc.scalar.activation(row_factor, s_inverse[:], ACT.Sqrt, scale=GRAD_FACTOR * GRAD_FACTOR)
        for h in range(2):
            nc.vector.tensor_tensor(placed[:].indirect(offsets[:, pages[h]]), u[:, halves[h]], u_mean_neg[:, halves[h]], ALU.add)
        for c in range(len(OUT_CUTS) - 1):
            cols = slice(OUT_CUTS[c], OUT_CUTS[c + 1])
            nc.vector.scalar_tensor_tensor(total[:, cols], placed[:, cols], row_factor, total[:, cols], ALU.mult, ALU.add)
            nc.sync.dma_start(out[:, cols], total[:, cols])
